import numpy as np
CORES = [65,73,81,89,97,105,113,121,193,201,209,217,225,233,241,249]
N = 16
ROOT = 1
def setup_inputs(rng):
    return {"x": rng.standard_normal((N, 128, N * 16), dtype=np.float32)}
def reference(x):
    return {"y": np.stack([x[ROOT][:, r * 16:(r + 1) * 16] for r in range(N)])}

@@ -1,0 +1,77 @@
+import concourse.bass as bass
+
+BLK = 16
+SPAN = 3
+
+SCRATCH = {
+    "xs": ("sbuf", [128, 256], "float32"),
+    "part": ("sbuf", [128, SPAN * BLK], "float32"),
+    "land": ("dram", [128, BLK], "float32"),
+}
+SEMAPHORES = ["loaded", "sent", "arrived", "stored"]
+
+HELPERS = (2, 3, 6, 7)
+
+
+def bits(mask):
+    return bin(mask).count("1")
+
+
+def design(T, topo):
+    root = T.cores[T.root]
+    base = root - root % 8
+    far = [r for r, c in enumerate(T.cores) if not topo.may_write(root, c)]
+    near = [r for r, c in enumerate(T.cores) if topo.may_write(root, c) and c != root]
+    stage1, stage2 = [], {}
+    for q, h in enumerate(HELPERS):
+        a, b = far[2 * q], far[2 * q + 1]
+        stage1.append((base + h, a, 0xF << (4 * q)))
+        stage2[base + h] = [(a, 0, 0x0F), (b, (b - a) * BLK, 0xF0)]
+    direct = [(r, 1 << i) for i, r in enumerate(near)]
+    return root, stage1, stage2, direct
+
+
+def send(g, core, T, topo, items, local_sem):
+    trs = []
+    for dst, out, src, mask in items:
+        rid, pid = topo.addr(dst, core)
+        trs.append(bass.RemoteDMATransfer(dst_ids=[bass.DstId(rid=rid, pnc=pid)], dma_engine_mask=mask,
+                                          remote_sem=T.sem.arrived, src=src, dst=out))
+    g.remote_dma_fused(trs, local_sem=local_sem)
+    return sum(bits(it[3]) for it in items)
+
+
+def rank_program(g, core, T, topo):
+    root, stage1, stage2, direct = design(T, topo)
+    rank = T.rank_of(core)
+
+    if core == root:
+        g.dma_start(T.xs[:, :], T.x[:, :]).then_inc(T.sem.loaded, 16)
+        g.wait_ge(T.sem.loaded, 16)
+        n = send(g, core, T, topo,
+                 [(h, T.part[:, :], T.xs[:, a * BLK:(a + SPAN) * BLK], m) for h, a, m in stage1], T.sem.sent)
+        n += send(g, core, T, topo,
+                  [(T.cores[r], T.land[:, :], T.xs[:, r * BLK:(r + 1) * BLK], m) for r, m in direct], T.sem.sent)
+        g.dma_start(T.y[:, :], T.xs[:, rank * BLK:(rank + 1) * BLK]).then_inc(T.sem.stored, 16)
+        g.wait_ge(T.sem.stored, 16)
+        g.wait_ge(T.sem.sent, n)
+        return
+
+    if core in stage2:
+        mine = [m for h, a, m in stage1 if h == core][0]
+        g.wait_ge(T.sem.arrived, bits(mine))
+        n = send(g, core, T, topo,
+                 [(T.cores[r], T.land[:, :], T.part[:, c:c + BLK], m) for r, c, m in stage2[core]], T.sem.sent)
+        g.wait_ge(T.sem.sent, n)
+        return
+
+    if rank is None:
+        return
+
+    count = dict(direct)
+    for lst in stage2.values():
+        for r, c, m in lst:
+            count[r] = m
+    g.wait_ge(T.sem.arrived, bits(count[rank]))
+    g.dma_start(T.y[:, :], T.land[:, :]).then_inc(T.sem.stored, 16)
+    g.wait_ge(T.sem.stored, 16)

@@ -2,6 +2,7 @@ import concourse.bass as bass
 
 BLK = 16
 SPAN = 3
+MODE = "V5"
 
 SCRATCH = {
     "xs": ("sbuf", [128, 256], "float32"),
@@ -23,11 +24,22 @@ def design(T, topo):
     far = [r for r, c in enumerate(T.cores) if not topo.may_write(root, c)]
     near = [r for r, c in enumerate(T.cores) if topo.may_write(root, c) and c != root]
     stage1, stage2 = [], {}
+    relayed = []
     for q, h in enumerate(HELPERS):
         a, b = far[2 * q], far[2 * q + 1]
+        mid = a + 1
         stage1.append((base + h, a, 0xF << (4 * q)))
-        stage2[base + h] = [(a, 0, 0x0F), (b, (b - a) * BLK, 0xF0)]
-    direct = [(r, 1 << i) for i, r in enumerate(near)]
+        if MODE == "V1" or mid == T.root:
+            stage2[base + h] = [[(a, 0, 0x0F), (b, (b - a) * BLK, 0xF0)]]
+        elif MODE == "V4":
+            stage2[base + h] = [[(a, 0, 0x0F), (b, (b - a) * BLK, 0x30), (mid, BLK, 0xC0)]]
+            relayed.append(mid)
+        elif MODE == "V5":
+            stage2[base + h] = [[(a, 0, 0x0F), (b, (b - a) * BLK, 0xF0)], [(mid, BLK, 0xFF)]]
+            relayed.append(mid)
+    left = [r for r in near if r not in relayed]
+    k = 8 // len(left) if len(left) in (1, 2, 4, 8) else 1
+    direct = [(r, ((1 << k) - 1) << (k * i)) for i, r in enumerate(left)]
     return root, stage1, stage2, direct
 
 
@@ -60,8 +72,10 @@ def rank_program(g, core, T, topo):
     if core in stage2:
         mine = [m for h, a, m in stage1 if h == core][0]
         g.wait_ge(T.sem.arrived, bits(mine))
-        n = send(g, core, T, topo,
-                 [(T.cores[r], T.land[:, :], T.part[:, c:c + BLK], m) for r, c, m in stage2[core]], T.sem.sent)
+        n = 0
+        for call in stage2[core]:
+            n += send(g, core, T, topo,
+                      [(T.cores[r], T.land[:, :], T.part[:, c:c + BLK], m) for r, c, m in call], T.sem.sent)
         g.wait_ge(T.sem.sent, n)
         return
 
@@ -69,9 +83,10 @@ def rank_program(g, core, T, topo):
         return
 
     count = dict(direct)
-    for lst in stage2.values():
-        for r, c, m in lst:
-            count[r] = m
+    for calls in stage2.values():
+        for call in calls:
+            for r, c, m in call:
+                count[r] = m
     g.wait_ge(T.sem.arrived, bits(count[rank]))
     g.dma_start(T.y[:, :], T.land[:, :]).then_inc(T.sem.stored, 16)
     g.wait_ge(T.sem.stored, 16)

@@ -2,7 +2,6 @@ import concourse.bass as bass
 
 BLK = 16
 SPAN = 3
-MODE = "V5"
 
 SCRATCH = {
     "xs": ("sbuf", [128, 256], "float32"),
@@ -23,33 +22,27 @@ def design(T, topo):
     base = root - root % 8
     far = [r for r, c in enumerate(T.cores) if not topo.may_write(root, c)]
     near = [r for r, c in enumerate(T.cores) if topo.may_write(root, c) and c != root]
-    stage1, stage2 = [], {}
-    relayed = []
+    stage1, stage2, relayed = [], {}, []
     for q, h in enumerate(HELPERS):
         a, b = far[2 * q], far[2 * q + 1]
         mid = a + 1
         stage1.append((base + h, a, 0xF << (4 * q)))
-        if MODE == "V1" or mid == T.root:
-            stage2[base + h] = [[(a, 0, 0x0F), (b, (b - a) * BLK, 0xF0)]]
-        elif MODE == "V4":
-            stage2[base + h] = [[(a, 0, 0x0F), (b, (b - a) * BLK, 0x30), (mid, BLK, 0xC0)]]
-            relayed.append(mid)
-        elif MODE == "V5":
-            stage2[base + h] = [[(a, 0, 0x0F), (b, (b - a) * BLK, 0xF0)], [(mid, BLK, 0xFF)]]
+        stage2[base + h] = [[(a, 0, 0x0F), (b, (b - a) * BLK, 0xF0)]]
+        if mid != T.root:
+            stage2[base + h].append([(mid, BLK, 0xFF)])
             relayed.append(mid)
     left = [r for r in near if r not in relayed]
-    k = 8 // len(left) if len(left) in (1, 2, 4, 8) else 1
-    direct = [(r, ((1 << k) - 1) << (k * i)) for i, r in enumerate(left)]
+    direct = [(r, 0x3 << (2 * i)) for i, r in enumerate(left)]
     return root, stage1, stage2, direct
 
 
-def send(g, core, T, topo, items, local_sem):
+def send(g, core, T, topo, items):
     trs = []
     for dst, out, src, mask in items:
         rid, pid = topo.addr(dst, core)
         trs.append(bass.RemoteDMATransfer(dst_ids=[bass.DstId(rid=rid, pnc=pid)], dma_engine_mask=mask,
                                           remote_sem=T.sem.arrived, src=src, dst=out))
-    g.remote_dma_fused(trs, local_sem=local_sem)
+    g.remote_dma_fused(trs, local_sem=T.sem.sent)
     return sum(bits(it[3]) for it in items)
 
 
@@ -61,9 +54,9 @@ def rank_program(g, core, T, topo):
         g.dma_start(T.xs[:, :], T.x[:, :]).then_inc(T.sem.loaded, 16)
         g.wait_ge(T.sem.loaded, 16)
         n = send(g, core, T, topo,
-                 [(h, T.part[:, :], T.xs[:, a * BLK:(a + SPAN) * BLK], m) for h, a, m in stage1], T.sem.sent)
+                 [(h, T.part[:, :], T.xs[:, a * BLK:(a + SPAN) * BLK], m) for h, a, m in stage1])
         n += send(g, core, T, topo,
-                  [(T.cores[r], T.land[:, :], T.xs[:, r * BLK:(r + 1) * BLK], m) for r, m in direct], T.sem.sent)
+                  [(T.cores[r], T.land[:, :], T.xs[:, r * BLK:(r + 1) * BLK], m) for r, m in direct])
         g.dma_start(T.y[:, :], T.xs[:, rank * BLK:(rank + 1) * BLK]).then_inc(T.sem.stored, 16)
         g.wait_ge(T.sem.stored, 16)
         g.wait_ge(T.sem.sent, n)
@@ -75,18 +68,18 @@ def rank_program(g, core, T, topo):
         n = 0
         for call in stage2[core]:
             n += send(g, core, T, topo,
-                      [(T.cores[r], T.land[:, :], T.part[:, c:c + BLK], m) for r, c, m in call], T.sem.sent)
+                      [(T.cores[r], T.land[:, :], T.part[:, c:c + BLK], m) for r, c, m in call])
         g.wait_ge(T.sem.sent, n)
         return
 
     if rank is None:
         return
 
-    count = dict(direct)
+    engines = dict(direct)
     for calls in stage2.values():
         for call in calls:
             for r, c, m in call:
-                count[r] = m
-    g.wait_ge(T.sem.arrived, bits(count[rank]))
+                engines[r] = m
+    g.wait_ge(T.sem.arrived, bits(engines[rank]))
     g.dma_start(T.y[:, :], T.land[:, :]).then_inc(T.sem.stored, 16)
     g.wait_ge(T.sem.stored, 16)

import concourse.bass as bass

BLK = 16
SPAN = 3

SCRATCH = {
    "xs": ("sbuf", [128, 256], "float32"),
    "part": ("sbuf", [128, SPAN * BLK], "float32"),
    "land": ("dram", [128, BLK], "float32"),
}
SEMAPHORES = ["loaded", "sent", "arrived", "stored"]

HELPERS = (2, 3, 6, 7)


def bits(mask):
    return bin(mask).count("1")


def design(T, topo):
    root = T.cores[T.root]
    base = root - root % 8
    far = [r for r, c in enumerate(T.cores) if not topo.may_write(root, c)]
    near = [r for r, c in enumerate(T.cores) if topo.may_write(root, c) and c != root]
    stage1, stage2, relayed = [], {}, []
    for q, h in enumerate(HELPERS):
        a, b = far[2 * q], far[2 * q + 1]
        mid = a + 1
        stage1.append((base + h, a, 0xF << (4 * q)))
        stage2[base + h] = [[(a, 0, 0x0F), (b, (b - a) * BLK, 0xF0)]]
        if mid != T.root:
            stage2[base + h].append([(mid, BLK, 0xFF)])
            relayed.append(mid)
    left = [r for r in near if r not in relayed]
    direct = [(r, 0x3 << (2 * i)) for i, r in enumerate(left)]
    return root, stage1, stage2, direct


def send(g, core, T, topo, items):
    trs = []
    for dst, out, src, mask in items:
        rid, pid = topo.addr(dst, core)
        trs.append(bass.RemoteDMATransfer(dst_ids=[bass.DstId(rid=rid, pnc=pid)], dma_engine_mask=mask,
                                          remote_sem=T.sem.arrived, src=src, dst=out))
    g.remote_dma_fused(trs, local_sem=T.sem.sent)
    return sum(bits(it[3]) for it in items)


def rank_program(g, core, T, topo):
    root, stage1, stage2, direct = design(T, topo)
    rank = T.rank_of(core)

    if core == root:
        g.dma_start(T.xs[:, :], T.x[:, :]).then_inc(T.sem.loaded, 16)
        g.wait_ge(T.sem.loaded, 16)
        n = send(g, core, T, topo,
                 [(h, T.part[:, :], T.xs[:, a * BLK:(a + SPAN) * BLK], m) for h, a, m in stage1])
        n += send(g, core, T, topo,
                  [(T.cores[r], T.land[:, :], T.xs[:, r * BLK:(r + 1) * BLK], m) for r, m in direct])
        g.dma_start(T.y[:, :], T.xs[:, rank * BLK:(rank + 1) * BLK]).then_inc(T.sem.stored, 16)
        g.wait_ge(T.sem.stored, 16)
        g.wait_ge(T.sem.sent, n)
        return

    if core in stage2:
        mine = [m for h, a, m in stage1 if h == core][0]
        g.wait_ge(T.sem.arrived, bits(mine))
        n = 0
        for call in stage2[core]:
            n += send(g, core, T, topo,
                      [(T.cores[r], T.land[:, :], T.part[:, c:c + BLK], m) for r, c, m in call])
        g.wait_ge(T.sem.sent, n)
        return

    if rank is None:
        return

    engines = dict(direct)
    for calls in stage2.values():
        for call in calls:
            for r, c, m in call:
                engines[r] = m
    g.wait_ge(T.sem.arrived, bits(engines[rank]))
    g.dma_start(T.y[:, :], T.land[:, :]).then_inc(T.sem.stored, 16)
    g.wait_ge(T.sem.stored, 16)
